import numpy as np
import ml_dtypes


def mxq(x, axis, fmt="e4m3"):
    dtype, down = {"e4m3": (ml_dtypes.float8_e4m3fn, 7), "e5m2": (ml_dtypes.float8_e5m2, 14)}[fmt]
    v = np.moveaxis(np.asarray(x, np.float32).astype(ml_dtypes.bfloat16).astype(np.float64), axis, -1)
    blocks = v.reshape(v.shape[:-1] + (-1, 32))
    amax = np.abs(blocks).max(-1, keepdims=True)
    byte = np.maximum(np.where(amax > 0, np.frexp(amax)[1] - 1 + 127, 0) - down, 1)
    scale = np.exp2(byte - 127.0)
    codes = (blocks / scale).astype(np.float32).astype(dtype).astype(np.float64)
    return np.moveaxis((codes * scale).reshape(v.shape), -1, axis)


WIDE = False


def mx_kscale(k):
    if not WIDE:
        return np.ones(k)
    levels = np.array([10, -10, 5, -5, 0])
    if k % 512:
        return np.exp2(np.random.permutation(np.resize(levels, k // 32))).repeat(32)
    a = np.empty((k // 512, 16))
    for p in range(k // 512):
        a[p, :8] = np.random.permutation(np.resize(levels, 8))
        for g in range(8):
            far = levels[np.abs(levels - a[p, g]) >= 10]
            a[p, g + 8] = far[np.random.randint(len(far))]
    return np.exp2(a.ravel()).repeat(32)


def f64(x):
    return np.asarray(x).astype(np.float64)


def striped(idx):
    return np.tile(idx.reshape(-1, 16).T, (8, 1)).astype(np.uint16)


def unstriped(offs):
    return offs[:16].T.reshape(-1).astype(np.int64)


def sigmoid(v):
    return 1.0 / (1.0 + np.exp(-np.maximum(v, -700.0)))


K, T, E, C, H, N = 1024, 512, 4, 128, 1024, 128


def by_expert(wq, xq):
    return np.concatenate([wq[e].T @ xq[:, e * C:(e + 1) * C] for e in range(E)], axis=1)


def setup_inputs():
    n = np.random.standard_normal
    s = mx_kscale(K)[:, None]
    u = mx_kscale(H)
    return {
        "xT": (n((K, T)) * s).astype(np.float32),
        "w1": (n((E, K, H)) / np.sqrt(K) / s[None]).astype(np.float32),
        "w3": (n((E, K, H)) / np.sqrt(K) / s[None] * u[None, None, :]).astype(np.float32),
        "w2": (n((E, H, N)) / np.sqrt(H) / u[None, :, None]).astype(np.float32),
        "gate": np.tile(np.random.uniform(0.2, 1.0, E * C), (N, 1)).astype(np.float32),
        "offs": striped(np.random.permutation(T)[:E * C]),
    }


def reference(xT, w1, w3, w2, gate, offs):
    idx = unstriped(offs)
    xq = mxq(f64(xT)[:, idx], 0, "e4m3")
    h = sigmoid(by_expert(mxq(f64(w1), 1, "e4m3"), xq))
    h = h * by_expert(mxq(f64(w3), 1, "e4m3"), xq)
    y = by_expert(mxq(f64(w2), 1, "e4m3"), mxq(h, 0, "e4m3"))
    out = np.zeros((N, T))
    out[:, idx] = f64(gate) * y
    return out

@@ -1,0 +1,176 @@
+from contextlib import ExitStack
+
+import concourse.mybir as mybir
+
+K, T, E, C, H, N = 1024, 512, 4, 128, 1024, 128
+FLOPS = 2 * E * C * (2 * K * H + H * N)
+
+F32 = mybir.dt.float32
+BF16 = mybir.dt.bfloat16
+U32 = mybir.dt.uint32
+U16 = mybir.dt.uint16
+U8 = mybir.dt.uint8
+FP8X4 = mybir.dt.float8_e4m3fn_x4
+MULT = mybir.AluOpType.mult
+SIGMOID = mybir.ActivationFunctionType.Sigmoid
+
+P = 128
+J = 4
+PASS = P * J
+G = K // PASS
+B = H // PASS
+
+
+def tile_routed_moe_kernel(tc, xT, w1, w3, w2, gate, offs, out):
+    nc = tc.nc
+
+    with ExitStack() as ctx:
+        keep = ctx.enter_context(tc.tile_pool(name="keep", bufs=1))
+        raws = ctx.enter_context(tc.tile_pool(name="raws", bufs=6))
+        groups = ctx.enter_context(tc.tile_pool(name="groups", bufs=3))
+        weights = ctx.enter_context(tc.tile_pool(name="weights", bufs=3))
+        work = ctx.enter_context(tc.tile_pool(name="work", bufs=3))
+        psum = ctx.enter_context(tc.psum_pool(name="psum", bufs=2))
+
+        offsets = keep.tile([P, E * C // 16], U16, name="offsets")
+        gates = keep.tile([P, E * C], F32, name="gates")
+        window = keep.tile([P, T], F32, name="window")
+        slot_codes = keep.tile([P, G, E * C], U32, name="slot_codes", align_bytes=64)
+        slot_scales = keep.tile([P, G, E * C], U8, name="slot_scales", align_bytes=64)
+
+        def copy_on(engine, dst, src):
+            if engine == 0:
+                nc.vector.tensor_copy(dst, src)
+            else:
+                nc.scalar.copy(dst, src)
+
+        token_codes, token_scales, token_raw = [], [], []
+        for g in range(G):
+            codes = keep.tile([P, T], U32, name=f"token_codes{g}", align_bytes=64)
+            scales = keep.tile([P, T], U8, name=f"token_scales{g}", align_bytes=64)
+            nc.gpsimd.memset(scales[:], 0)
+            token_codes.append(codes)
+            token_scales.append(scales)
+            raw = raws.tile([P, J, T], F32, name="raw")
+            nc.sync.dma_start(out=raw[:], in_=xT.rearrange("(g p j) n -> g p j n", p=P, j=J)[g])
+            token_raw.append(raw)
+            if g == 0:
+                nc.sync.dma_start(offsets[:], offs)
+        for g in range(G):
+            grouped = keep.tile([P, T, J], BF16, name=f"token_grouped{g}", align_bytes=64)
+            copy_on(g, grouped[:].rearrange("p (c i) j -> p c j i", i=4),
+                    token_raw[g][:].rearrange("p j (c i) -> p c j i", i=4))
+            nc.vector.quantize_mx(out=token_codes[g][:].bitcast(FP8X4), scales=token_scales[g][:],
+                                  in_=grouped[:].rearrange("p n j -> p (n j)"))
+        piece = 256
+        for s in range(E * C // piece):
+            cols = offsets[:, s * (piece // 16):(s + 1) * (piece // 16)]
+            for g in range(G):
+                nc.vector.tensor_copy(slot_codes[:, g, s * piece:(s + 1) * piece], token_codes[g][:].indirect(cols))
+                nc.vector.tensor_copy(slot_scales[:, g, s * piece:(s + 1) * piece], token_scales[g][:].indirect(cols))
+
+        def load(dram, g, c0, c1):
+            raw = raws.tile([P, J, c1 - c0], F32, name="raw")
+            nc.sync.dma_start(out=raw[:], in_=dram.rearrange("(g p j) c -> g p j c", p=P, j=J)[g][:, :, c0:c1])
+            return raw
+
+        def interleave(engine, grouped, raw, c0, m0, m1):
+            copy_on(engine, grouped[:].rearrange("p (t m j) -> p m j t", t=J, j=J)[:, m0:m1],
+                    raw[:, :, c0:c0 + J * (m1 - m0)].rearrange("p j (m t) -> p m j t", t=J))
+
+        def quantize(grouped, codes, scales, parts):
+            width = PASS // parts
+            for i in range(parts):
+                cols = slice(i * width, (i + 1) * width)
+                nc.vector.quantize_mx(out=codes[:, cols].bitcast(FP8X4), scales=scales[:, cols],
+                                      in_=grouped[:, i * width * J:(i + 1) * width * J])
+
+        def prepare(dram, name, last):
+            codes = weights.tile([P, G, H], U32, name=f"{name}_codes", align_bytes=64)
+            scales = weights.tile([P, G, H], U8, name=f"{name}_scales", align_bytes=64)
+            for g in range(G):
+                split = last and g == G - 1
+                if not split:
+                    raw = load(dram, g, 0, H)
+                for b in range(B):
+                    cols = slice(b * PASS, (b + 1) * PASS)
+                    grouped = groups.tile([P, PASS * J], BF16, name=f"grouped{b}", align_bytes=64)
+                    if not split:
+                        interleave(b, grouped, raw, b * PASS, 0, P)
+                    else:
+                        n = P // (b + 1)
+                        for m0 in range(0, P, n):
+                            raw = load(dram, g, b * PASS + J * m0, b * PASS + J * (m0 + n))
+                            cut = n * 5 // 8
+                            interleave(0, grouped, raw, 0, m0, m0 + cut)
+                            interleave(1, grouped, raw, J * cut, m0 + cut, m0 + n)
+                    quantize(grouped, codes[:, g, cols], scales[:, g, cols], 1 + b * split)
+            return codes, scales
+
+        def prepare_w2(e):
+            raw = raws.tile([P, B, J, N], F32, name="raw")
+            nc.sync.dma_start(out=raw[:], in_=w2[e].rearrange("(b p j) n -> p b j n", p=P, j=J))
+            codes = weights.tile([P, B, N], U32, name="w2_codes", align_bytes=64)
+            scales = weights.tile([P, B, N], U8, name="w2_scales", align_bytes=64)
+            grouped = groups.tile([P, B, N, J], BF16, name="w2_grouped", align_bytes=64)
+            for b in range(B):
+                copy_on(1 if e >= E - 2 else b, grouped[:, b].rearrange("p (c i) j -> p c j i", i=4),
+                        raw[:, b].rearrange("p j (c i) -> p c j i", i=4))
+            nc.vector.quantize_mx(out=codes[:].rearrange("p b n -> p (b n)").bitcast(FP8X4),
+                                  scales=scales[:].rearrange("p b n -> p (b n)"),
+                                  in_=grouped[:].rearrange("p b n j -> p (b n j)"))
+            return codes, scales
+
+        def hidden_sums(codes, scales, e, b, name):
+            acc = psum.tile([P, J, C], F32, name=name)
+            slots = slice(e * C, (e + 1) * C)
+            for t in range(J):
+                cols = slice(b * PASS + t * P, b * PASS + (t + 1) * P)
+                for g in range(G):
+                    nc.tensor.matmul_mx(
+                        out=acc[:, t, :],
+                        lhsT=codes[:, g, cols].bitcast(FP8X4), lhsT_scale=scales[:, g, cols],
+                        rhs=slot_codes[:, g, slots].bitcast(FP8X4), rhs_scale=slot_scales[:, g, slots],
+                        start=(g == 0), stop=(g == G - 1))
+            return acc
+
+        def second_layer(e, c2, s2, h_codes, h_scales):
+            y = psum.tile([N, C], F32, name="y")
+            for b in range(B):
+                nc.tensor.matmul_mx(
+                    out=y[:],
+                    lhsT=c2[:, b, :].bitcast(FP8X4), lhsT_scale=s2[:, b, :],
+                    rhs=h_codes[:, b, :].bitcast(FP8X4), rhs_scale=h_scales[:, b, :],
+                    start=(b == 0), stop=(b == B - 1))
+            y_sb = work.tile([N, C], F32, name="y_sb")
+            nc.scalar.copy(y_sb[:], y[:])
+            nc.vector.tensor_tensor(window[:].indirect(offsets[:, e * (C // 16):(e + 1) * (C // 16)]),
+                                    y_sb[:], gates[:, e * C:(e + 1) * C], MULT)
+
+        waiting = []
+        for e in range(E):
+            c1, s1 = prepare(w1[e], "w1", False)
+            c3, s3 = prepare(w3[e], "w3", e == E - 1)
+            if e == 0:
+                nc.sync.dma_start(gates[:], gate)
+            if e != E - 2:
+                c2, s2 = prepare_w2(e)
+            h_codes = work.tile([P, B, C], U32, name="h_codes", align_bytes=64)
+            h_scales = work.tile([P, B, C], U8, name="h_scales", align_bytes=64)
+            for b in range(B):
+                a = hidden_sums(c1, s1, e, b, "a")
+                sig = work.tile([P, J, C], F32, name="sig")
+                nc.scalar.activation(sig[:], a[:], SIGMOID)
+                v = hidden_sums(c3, s3, e, b, "v")
+                h = work.tile([P, C, J], BF16, name="h", align_bytes=64)
+                nc.vector.tensor_tensor(h[:], v[:].rearrange("p t n -> p n t"), sig[:].rearrange("p t n -> p n t"), MULT)
+                nc.vector.quantize_mx(out=h_codes[:, b, :].bitcast(FP8X4), scales=h_scales[:, b, :],
+                                      in_=h[:].rearrange("p n t -> p (n t)"))
+            if e == E - 2:
+                waiting.append((e, h_codes, h_scales))
+            else:
+                for late, l_codes, l_scales in waiting:
+                    lc2, ls2 = prepare_w2(late)
+                    second_layer(late, lc2, ls2, l_codes, l_scales)
+                second_layer(e, c2, s2, h_codes, h_scales)
+        nc.sync.dma_start(out, window[:])

@@ -69,59 +69,73 @@ def tile_routed_moe_kernel(tc, xT, w1, w3, w2, gate, offs, out):
                 nc.vector.tensor_copy(slot_codes[:, g, s * piece:(s + 1) * piece], token_codes[g][:].indirect(cols))
                 nc.vector.tensor_copy(slot_scales[:, g, s * piece:(s + 1) * piece], token_scales[g][:].indirect(cols))
 
-        def load(dram, g, c0, c1):
-            raw = raws.tile([P, J, c1 - c0], F32, name="raw")
-            nc.sync.dma_start(out=raw[:], in_=dram.rearrange("(g p j) c -> g p j c", p=P, j=J)[g][:, :, c0:c1])
+        def load_pass(dram, g, cols=slice(0, H)):
+            raw = raws.tile([P, J, cols.stop - cols.start], F32, name="raw")
+            nc.sync.dma_start(out=raw[:], in_=dram.rearrange("(g p j) c -> g p j c", p=P, j=J)[g][:, :, cols])
             return raw
 
         def interleave(engine, grouped, raw, c0, m0, m1):
             copy_on(engine, grouped[:].rearrange("p (t m j) -> p m j t", t=J, j=J)[:, m0:m1],
-                    raw[:, :, c0:c0 + J * (m1 - m0)].rearrange("p j (m t) -> p m j t", t=J))
+                    raw[:, :, c0 + J * m0:c0 + J * m1].rearrange("p j (m t) -> p m j t", t=J))
 
-        def quantize(grouped, codes, scales, parts):
+        def quantize(grouped, codes, scales, c0, parts):
             width = PASS // parts
             for i in range(parts):
-                cols = slice(i * width, (i + 1) * width)
+                cols = slice(c0 + i * width, c0 + (i + 1) * width)
                 nc.vector.quantize_mx(out=codes[:, cols].bitcast(FP8X4), scales=scales[:, cols],
                                       in_=grouped[:, i * width * J:(i + 1) * width * J])
 
-        def prepare(dram, name, last):
+        def new_operand(name):
             codes = weights.tile([P, G, H], U32, name=f"{name}_codes", align_bytes=64)
             scales = weights.tile([P, G, H], U8, name=f"{name}_scales", align_bytes=64)
-            for g in range(G):
-                split = last and g == G - 1
-                if not split:
-                    raw = load(dram, g, 0, H)
-                for b in range(B):
-                    cols = slice(b * PASS, (b + 1) * PASS)
-                    grouped = groups.tile([P, PASS * J], BF16, name=f"grouped{b}", align_bytes=64)
-                    if not split:
-                        interleave(b, grouped, raw, b * PASS, 0, P)
-                    else:
-                        n = P // (b + 1)
-                        for m0 in range(0, P, n):
-                            raw = load(dram, g, b * PASS + J * m0, b * PASS + J * (m0 + n))
-                            cut = n * 5 // 8
-                            interleave(0, grouped, raw, 0, m0, m0 + cut)
-                            interleave(1, grouped, raw, J * cut, m0 + cut, m0 + n)
-                    quantize(grouped, codes[:, g, cols], scales[:, g, cols], 1 + b * split)
             return codes, scales
 
-        def prepare_w2(e):
+        def block(raw, c0, b, cut):
+            grouped = groups.tile([P, PASS * J], BF16, name=f"grouped{b}", align_bytes=64)
+            if cut > 0:
+                interleave(0, grouped, raw, c0, 0, cut)
+            if cut < P:
+                interleave(1, grouped, raw, c0, cut, P)
+            return grouped
+
+        def quantize_pass(grouped, operand, g, b, parts):
+            quantize(grouped, operand[0][:, g], operand[1][:, g], b * PASS, parts)
+
+        def whole_pass(dram, operand, g, cuts):
+            raw = load_pass(dram, g)
+            blocks = [block(raw, b * PASS, b, cuts[b]) for b in range(B)]
+            for b in range(B):
+                quantize_pass(blocks[b], operand, g, b, 1)
+
+        def load_w2(e):
             raw = raws.tile([P, B, J, N], F32, name="raw")
             nc.sync.dma_start(out=raw[:], in_=w2[e].rearrange("(b p j) n -> p b j n", p=P, j=J))
+            return raw
+
+        def interleave_w2(raw, b, engine):
+            grouped = groups.tile([P, N, J], BF16, name=f"w2_grouped{b}", align_bytes=64)
+            copy_on(engine, grouped[:].rearrange("p (c i) j -> p c j i", i=4),
+                    raw[:, b].rearrange("p j (c i) -> p c j i", i=4))
+            return grouped
+
+        def new_w2():
             codes = weights.tile([P, B, N], U32, name="w2_codes", align_bytes=64)
             scales = weights.tile([P, B, N], U8, name="w2_scales", align_bytes=64)
-            grouped = groups.tile([P, B, N, J], BF16, name="w2_grouped", align_bytes=64)
-            for b in range(B):
-                copy_on(1 if e >= E - 2 else b, grouped[:, b].rearrange("p (c i) j -> p c j i", i=4),
-                        raw[:, b].rearrange("p j (c i) -> p c j i", i=4))
-            nc.vector.quantize_mx(out=codes[:].rearrange("p b n -> p (b n)").bitcast(FP8X4),
-                                  scales=scales[:].rearrange("p b n -> p (b n)"),
-                                  in_=grouped[:].rearrange("p b n j -> p (b n j)"))
             return codes, scales
 
-        def hidden_sums(codes, scales, e, b, name):
+        def quantize_w2(grouped, operand, b):
+            nc.vector.quantize_mx(out=operand[0][:, b].bitcast(FP8X4), scales=operand[1][:, b],
+                                  in_=grouped[:].rearrange("p n j -> p (n j)"))
+
+        def prepare_w2(e):
+            raw, operand = load_w2(e), new_w2()
+            blocks = [interleave_w2(raw, b, b) for b in range(B)]
+            for b in range(B):
+                quantize_w2(blocks[b], operand, b)
+            return operand
+
+        def hidden_sums(operand, e, b, name):
+            codes, scales = operand
             acc = psum.tile([P, J, C], F32, name=name)
             slots = slice(e * C, (e + 1) * C)
             for t in range(J):
@@ -134,43 +148,64 @@ def tile_routed_moe_kernel(tc, xT, w1, w3, w2, gate, offs, out):
                         start=(g == 0), stop=(g == G - 1))
             return acc
 
-        def second_layer(e, c2, s2, h_codes, h_scales):
+        def open_gates(operand, e, b):
+            a = hidden_sums(operand, e, b, "a")
+            sig = work.tile([P, J, C], F32, name=f"sig{b}")
+            nc.scalar.activation(sig[:], a[:], SIGMOID)
+            return sig
+
+        def product(v, sig):
+            h = work.tile([P, C, J], BF16, name="h", align_bytes=64)
+            nc.vector.tensor_tensor(h[:], v[:].rearrange("p t n -> p n t"), sig[:].rearrange("p t n -> p n t"), MULT)
+            return h
+
+        def quantize_hidden(h, h_operand, b):
+            nc.vector.quantize_mx(out=h_operand[0][:, b, :].bitcast(FP8X4), scales=h_operand[1][:, b, :],
+                                  in_=h[:].rearrange("p n t -> p (n t)"))
+
+        def second_sums(w2_operand, h_operand):
             y = psum.tile([N, C], F32, name="y")
             for b in range(B):
                 nc.tensor.matmul_mx(
                     out=y[:],
-                    lhsT=c2[:, b, :].bitcast(FP8X4), lhsT_scale=s2[:, b, :],
-                    rhs=h_codes[:, b, :].bitcast(FP8X4), rhs_scale=h_scales[:, b, :],
+                    lhsT=w2_operand[0][:, b, :].bitcast(FP8X4), lhsT_scale=w2_operand[1][:, b, :],
+                    rhs=h_operand[0][:, b, :].bitcast(FP8X4), rhs_scale=h_operand[1][:, b, :],
                     start=(b == 0), stop=(b == B - 1))
             y_sb = work.tile([N, C], F32, name="y_sb")
             nc.scalar.copy(y_sb[:], y[:])
+            return y_sb
+
+        def scatter(e, y_sb):
             nc.vector.tensor_tensor(window[:].indirect(offsets[:, e * (C // 16):(e + 1) * (C // 16)]),
                                     y_sb[:], gates[:, e * C:(e + 1) * C], MULT)
 
-        waiting = []
+        def new_hidden(e):
+            codes = keep.tile([P, B, C], U32, name=f"h_codes{e}", align_bytes=64)
+            scales = keep.tile([P, B, C], U8, name=f"h_scales{e}", align_bytes=64)
+            return codes, scales
+
+        def prepare_late(e, engines):
+            raw, operand = load_w2(e), new_w2()
+            for b in range(B):
+                quantize_w2(interleave_w2(raw, b, engines[b]), operand, b)
+            return operand
+
+        late = []
         for e in range(E):
-            c1, s1 = prepare(w1[e], "w1", False)
-            c3, s3 = prepare(w3[e], "w3", e == E - 1)
+            op1, op3, h_op = new_operand("w1"), new_operand("w3"), new_hidden(e)
+            for g in range(G):
+                whole_pass(w1[e], op1, g, (P, 0))
+            sigs = [open_gates(op1, e, b) for b in range(B)]
+            for g in range(G):
+                whole_pass(w3[e], op3, g, (80, 88) if (e, g) == (E - 1, G - 1) else (P, 0))
             if e == 0:
                 nc.sync.dma_start(gates[:], gate)
-            if e != E - 2:
-                c2, s2 = prepare_w2(e)
-            h_codes = work.tile([P, B, C], U32, name="h_codes", align_bytes=64)
-            h_scales = work.tile([P, B, C], U8, name="h_scales", align_bytes=64)
             for b in range(B):
-                a = hidden_sums(c1, s1, e, b, "a")
-                sig = work.tile([P, J, C], F32, name="sig")
-                nc.scalar.activation(sig[:], a[:], SIGMOID)
-                v = hidden_sums(c3, s3, e, b, "v")
-                h = work.tile([P, C, J], BF16, name="h", align_bytes=64)
-                nc.vector.tensor_tensor(h[:], v[:].rearrange("p t n -> p n t"), sig[:].rearrange("p t n -> p n t"), MULT)
-                nc.vector.quantize_mx(out=h_codes[:, b, :].bitcast(FP8X4), scales=h_scales[:, b, :],
-                                      in_=h[:].rearrange("p n t -> p (n t)"))
-            if e == E - 2:
-                waiting.append((e, h_codes, h_scales))
+                quantize_hidden(product(hidden_sums(op3, e, b, "v"), sigs[b]), h_op, b)
+            if e < 2:
+                scatter(e, second_sums(prepare_w2(e), h_op))
             else:
-                for late, l_codes, l_scales in waiting:
-                    lc2, ls2 = prepare_w2(late)
-                    second_layer(late, lc2, ls2, l_codes, l_scales)
-                second_layer(e, c2, s2, h_codes, h_scales)
+                late.append((e, h_op))
+        for e, h_op in late:
+            scatter(e, second_sums(prepare_late(e, (1, 1)), h_op))
         nc.sync.dma_start(out, window[:])

@@ -51,15 +51,15 @@ def tile_routed_moe_kernel(tc, xT, w1, w3, w2, gate, offs, out):
             nc.gpsimd.memset(scales[:], 0)
             token_codes.append(codes)
             token_scales.append(scales)
-            raw = raws.tile([P, J, T], F32, name="raw")
-            nc.sync.dma_start(out=raw[:], in_=xT.rearrange("(g p j) n -> g p j n", p=P, j=J)[g])
-            token_raw.append(raw)
+            raw = raws.tile([P, J * T], F32, name="raw")
+            nc.sync.dma_start(out=raw[:], in_=xT.rearrange("(g p j) n -> g p (j n)", p=P, j=J)[g])
+            token_raw.append(raw[:].rearrange("p (j n) -> p j n", j=J))
             if g == 0:
                 nc.sync.dma_start(offsets[:], offs)
         for g in range(G):
             grouped = keep.tile([P, T, J], BF16, name=f"token_grouped{g}", align_bytes=64)
             copy_on(g, grouped[:].rearrange("p (c i) j -> p c j i", i=4),
-                    token_raw[g][:].rearrange("p j (c i) -> p c j i", i=4))
+                    token_raw[g].rearrange("p j (c i) -> p c j i", i=4))
             nc.vector.quantize_mx(out=token_codes[g][:].bitcast(FP8X4), scales=token_scales[g][:],
                                   in_=grouped[:].rearrange("p n j -> p (n j)"))
         piece = 256
@@ -69,10 +69,10 @@ def tile_routed_moe_kernel(tc, xT, w1, w3, w2, gate, offs, out):
                 nc.vector.tensor_copy(slot_codes[:, g, s * piece:(s + 1) * piece], token_codes[g][:].indirect(cols))
                 nc.vector.tensor_copy(slot_scales[:, g, s * piece:(s + 1) * piece], token_scales[g][:].indirect(cols))
 
-        def load_pass(dram, g, cols=slice(0, H)):
-            raw = raws.tile([P, J, cols.stop - cols.start], F32, name="raw")
-            nc.sync.dma_start(out=raw[:], in_=dram.rearrange("(g p j) c -> g p j c", p=P, j=J)[g][:, :, cols])
-            return raw
+        def load_pass(dram, g):
+            raw = raws.tile([P, J * H], F32, name="raw")
+            nc.sync.dma_start(out=raw[:], in_=dram.rearrange("(g p j) c -> g p (j c)", p=P, j=J)[g])
+            return raw[:].rearrange("p (j c) -> p j c", j=J)
 
         def interleave(engine, grouped, raw, c0, m0, m1):
             copy_on(engine, grouped[:].rearrange("p (t m j) -> p m j t", t=J, j=J)[:, m0:m1],
@@ -108,9 +108,9 @@ def tile_routed_moe_kernel(tc, xT, w1, w3, w2, gate, offs, out):
                 quantize_pass(blocks[b], operand, g, b, 1)
 
         def load_w2(e):
-            raw = raws.tile([P, B, J, N], F32, name="raw")
-            nc.sync.dma_start(out=raw[:], in_=w2[e].rearrange("(b p j) n -> p b j n", p=P, j=J))
-            return raw
+            raw = raws.tile([P, B, J * N], F32, name="raw")
+            nc.sync.dma_start(out=raw[:], in_=w2[e].rearrange("(b p j) n -> p b (j n)", p=P, j=J))
+            return raw[:].rearrange("p b (j n) -> p b j n", j=J)
 
         def interleave_w2(raw, b, engine):
             grouped = groups.tile([P, N, J], BF16, name=f"w2_grouped{b}", align_bytes=64)

from contextlib import ExitStack

import concourse.mybir as mybir

K, T, E, C, H, N = 1024, 512, 4, 128, 1024, 128
FLOPS = 2 * E * C * (2 * K * H + H * N)

F32 = mybir.dt.float32
BF16 = mybir.dt.bfloat16
U32 = mybir.dt.uint32
U16 = mybir.dt.uint16
U8 = mybir.dt.uint8
FP8X4 = mybir.dt.float8_e4m3fn_x4
MULT = mybir.AluOpType.mult
SIGMOID = mybir.ActivationFunctionType.Sigmoid

P = 128
J = 4
PASS = P * J
G = K // PASS
B = H // PASS


def tile_routed_moe_kernel(tc, xT, w1, w3, w2, gate, offs, out):
    nc = tc.nc

    with ExitStack() as ctx:
        keep = ctx.enter_context(tc.tile_pool(name="keep", bufs=1))
        raws = ctx.enter_context(tc.tile_pool(name="raws", bufs=6))
        groups = ctx.enter_context(tc.tile_pool(name="groups", bufs=3))
        weights = ctx.enter_context(tc.tile_pool(name="weights", bufs=3))
        work = ctx.enter_context(tc.tile_pool(name="work", bufs=3))
        psum = ctx.enter_context(tc.psum_pool(name="psum", bufs=2))

        offsets = keep.tile([P, E * C // 16], U16, name="offsets")
        gates = keep.tile([P, E * C], F32, name="gates")
        window = keep.tile([P, T], F32, name="window")
        slot_codes = keep.tile([P, G, E * C], U32, name="slot_codes", align_bytes=64)
        slot_scales = keep.tile([P, G, E * C], U8, name="slot_scales", align_bytes=64)

        def copy_on(engine, dst, src):
            if engine == 0:
                nc.vector.tensor_copy(dst, src)
            else:
                nc.scalar.copy(dst, src)

        token_codes, token_scales, token_raw = [], [], []
        for g in range(G):
            codes = keep.tile([P, T], U32, name=f"token_codes{g}", align_bytes=64)
            scales = keep.tile([P, T], U8, name=f"token_scales{g}", align_bytes=64)
            nc.gpsimd.memset(scales[:], 0)
            token_codes.append(codes)
            token_scales.append(scales)
            raw = raws.tile([P, J * T], F32, name="raw")
            nc.sync.dma_start(out=raw[:], in_=xT.rearrange("(g p j) n -> g p (j n)", p=P, j=J)[g])
            token_raw.append(raw[:].rearrange("p (j n) -> p j n", j=J))
            if g == 0:
                nc.sync.dma_start(offsets[:], offs)
        for g in range(G):
            grouped = keep.tile([P, T, J], BF16, name=f"token_grouped{g}", align_bytes=64)
            copy_on(g, grouped[:].rearrange("p (c i) j -> p c j i", i=4),
                    token_raw[g].rearrange("p j (c i) -> p c j i", i=4))
            nc.vector.quantize_mx(out=token_codes[g][:].bitcast(FP8X4), scales=token_scales[g][:],
                                  in_=grouped[:].rearrange("p n j -> p (n j)"))
        piece = 256
        for s in range(E * C // piece):
            cols = offsets[:, s * (piece // 16):(s + 1) * (piece // 16)]
            for g in range(G):
                nc.vector.tensor_copy(slot_codes[:, g, s * piece:(s + 1) * piece], token_codes[g][:].indirect(cols))
                nc.vector.tensor_copy(slot_scales[:, g, s * piece:(s + 1) * piece], token_scales[g][:].indirect(cols))

        def load_pass(dram, g):
            raw = raws.tile([P, J * H], F32, name="raw")
            nc.sync.dma_start(out=raw[:], in_=dram.rearrange("(g p j) c -> g p (j c)", p=P, j=J)[g])
            return raw[:].rearrange("p (j c) -> p j c", j=J)

        def interleave(engine, grouped, raw, c0, m0, m1):
            copy_on(engine, grouped[:].rearrange("p (t m j) -> p m j t", t=J, j=J)[:, m0:m1],
                    raw[:, :, c0 + J * m0:c0 + J * m1].rearrange("p j (m t) -> p m j t", t=J))

        def quantize(grouped, codes, scales, c0, parts):
            width = PASS // parts
            for i in range(parts):
                cols = slice(c0 + i * width, c0 + (i + 1) * width)
                nc.vector.quantize_mx(out=codes[:, cols].bitcast(FP8X4), scales=scales[:, cols],
                                      in_=grouped[:, i * width * J:(i + 1) * width * J])

        def new_operand(name):
            codes = weights.tile([P, G, H], U32, name=f"{name}_codes", align_bytes=64)
            scales = weights.tile([P, G, H], U8, name=f"{name}_scales", align_bytes=64)
            return codes, scales

        def block(raw, c0, b, cut):
            grouped = groups.tile([P, PASS * J], BF16, name=f"grouped{b}", align_bytes=64)
            if cut > 0:
                interleave(0, grouped, raw, c0, 0, cut)
            if cut < P:
                interleave(1, grouped, raw, c0, cut, P)
            return grouped

        def quantize_pass(grouped, operand, g, b, parts):
            quantize(grouped, operand[0][:, g], operand[1][:, g], b * PASS, parts)

        def whole_pass(dram, operand, g, cuts):
            raw = load_pass(dram, g)
            blocks = [block(raw, b * PASS, b, cuts[b]) for b in range(B)]
            for b in range(B):
                quantize_pass(blocks[b], operand, g, b, 1)

        def load_w2(e):
            raw = raws.tile([P, B, J * N], F32, name="raw")
            nc.sync.dma_start(out=raw[:], in_=w2[e].rearrange("(b p j) n -> p b (j n)", p=P, j=J))
            return raw[:].rearrange("p b (j n) -> p b j n", j=J)

        def interleave_w2(raw, b, engine):
            grouped = groups.tile([P, N, J], BF16, name=f"w2_grouped{b}", align_bytes=64)
            copy_on(engine, grouped[:].rearrange("p (c i) j -> p c j i", i=4),
                    raw[:, b].rearrange("p j (c i) -> p c j i", i=4))
            return grouped

        def new_w2():
            codes = weights.tile([P, B, N], U32, name="w2_codes", align_bytes=64)
            scales = weights.tile([P, B, N], U8, name="w2_scales", align_bytes=64)
            return codes, scales

        def quantize_w2(grouped, operand, b):
            nc.vector.quantize_mx(out=operand[0][:, b].bitcast(FP8X4), scales=operand[1][:, b],
                                  in_=grouped[:].rearrange("p n j -> p (n j)"))

        def prepare_w2(e):
            raw, operand = load_w2(e), new_w2()
            blocks = [interleave_w2(raw, b, b) for b in range(B)]
            for b in range(B):
                quantize_w2(blocks[b], operand, b)
            return operand

        def hidden_sums(operand, e, b, name):
            codes, scales = operand
            acc = psum.tile([P, J, C], F32, name=name)
            slots = slice(e * C, (e + 1) * C)
            for t in range(J):
                cols = slice(b * PASS + t * P, b * PASS + (t + 1) * P)
                for g in range(G):
                    nc.tensor.matmul_mx(
                        out=acc[:, t, :],
                        lhsT=codes[:, g, cols].bitcast(FP8X4), lhsT_scale=scales[:, g, cols],
                        rhs=slot_codes[:, g, slots].bitcast(FP8X4), rhs_scale=slot_scales[:, g, slots],
                        start=(g == 0), stop=(g == G - 1))
            return acc

        def open_gates(operand, e, b):
            a = hidden_sums(operand, e, b, "a")
            sig = work.tile([P, J, C], F32, name=f"sig{b}")
            nc.scalar.activation(sig[:], a[:], SIGMOID)
            return sig

        def product(v, sig):
            h = work.tile([P, C, J], BF16, name="h", align_bytes=64)
            nc.vector.tensor_tensor(h[:], v[:].rearrange("p t n -> p n t"), sig[:].rearrange("p t n -> p n t"), MULT)
            return h

        def quantize_hidden(h, h_operand, b):
            nc.vector.quantize_mx(out=h_operand[0][:, b, :].bitcast(FP8X4), scales=h_operand[1][:, b, :],
                                  in_=h[:].rearrange("p n t -> p (n t)"))

        def second_sums(w2_operand, h_operand):
            y = psum.tile([N, C], F32, name="y")
            for b in range(B):
                nc.tensor.matmul_mx(
                    out=y[:],
                    lhsT=w2_operand[0][:, b, :].bitcast(FP8X4), lhsT_scale=w2_operand[1][:, b, :],
                    rhs=h_operand[0][:, b, :].bitcast(FP8X4), rhs_scale=h_operand[1][:, b, :],
                    start=(b == 0), stop=(b == B - 1))
            y_sb = work.tile([N, C], F32, name="y_sb")
            nc.scalar.copy(y_sb[:], y[:])
            return y_sb

        def scatter(e, y_sb):
            nc.vector.tensor_tensor(window[:].indirect(offsets[:, e * (C // 16):(e + 1) * (C // 16)]),
                                    y_sb[:], gates[:, e * C:(e + 1) * C], MULT)

        def new_hidden(e):
            codes = keep.tile([P, B, C], U32, name=f"h_codes{e}", align_bytes=64)
            scales = keep.tile([P, B, C], U8, name=f"h_scales{e}", align_bytes=64)
            return codes, scales

        def prepare_late(e, engines):
            raw, operand = load_w2(e), new_w2()
            for b in range(B):
                quantize_w2(interleave_w2(raw, b, engines[b]), operand, b)
            return operand

        late = []
        for e in range(E):
            op1, op3, h_op = new_operand("w1"), new_operand("w3"), new_hidden(e)
            for g in range(G):
                whole_pass(w1[e], op1, g, (P, 0))
            sigs = [open_gates(op1, e, b) for b in range(B)]
            for g in range(G):
                whole_pass(w3[e], op3, g, (80, 88) if (e, g) == (E - 1, G - 1) else (P, 0))
            if e == 0:
                nc.sync.dma_start(gates[:], gate)
            for b in range(B):
                quantize_hidden(product(hidden_sums(op3, e, b, "v"), sigs[b]), h_op, b)
            if e < 2:
                scatter(e, second_sums(prepare_w2(e), h_op))
            else:
                late.append((e, h_op))
        for e, h_op in late:
            scatter(e, second_sums(prepare_late(e, (1, 1)), h_op))
        nc.sync.dma_start(out, window[:])
